import numpy as np, ml_dtypes
CORES = [6,15,38,47]
N = 4
BF = ml_dtypes.bfloat16
V, S, P, SH, RO = 1024, 4, 2, 2, 6
M, K1, K2, K3, K4, K5 = 4096, 1597, 613, 911, 1223, 74
def pack(s, li):
    return {"x": np.ascontiguousarray(s.reshape(N, 128, V)).astype(np.float32).astype(BF), "liar": np.ascontiguousarray(li).astype(np.int32)}
def states(rng):
    mid = rng.integers(30, 226, (N, 8, 16, 1)); wid = rng.integers(15, 90, (N, 8, 1, 1))
    return np.clip(np.rint(mid + wid * rng.standard_normal((N, 8, 16, V))), 0, 255).astype(np.int64)
def lies(rng, s, li):
    kind = rng.integers(0, 3, (N, 8, 1, V))
    w = np.where(kind == 0, 255 * rng.integers(0, 2, s.shape), np.where(kind == 1, 255 * rng.integers(0, 2, (N, 8, 1, V)), rng.integers(0, 256, s.shape)))
    return np.where(li[:, :, None, :], w, s)
def hit(u):
    return ((u * u >> 7) + u) & (M - 1)
def draws(i, c, t):
    m = np.arange(S, dtype=np.int64)[:, None]
    return hit((i * K1 + c * (K2 + K5 * m) + t * K3 + m * K4) & (M - 1))
def comps(rng, c):
    r = np.clip(np.rint(c[:, None, :] * 0.0625 + 50 * rng.standard_normal((8, 16, M))), 0, 255).astype(np.int64)
    left = c - np.add.reduce(r, axis=1)
    for i in rng.permutation(16):
        a = np.clip(left, -r[:, i], 255 - r[:, i]); r[:, i] += a; left = left - a
    return r
def steered(rng, us, m):
    c = np.full(M, M, np.int64); back = pow(K2 + K5 * m, 1023, M)
    for k in range(12):
        w = us[rng.integers(0, len(us), M)]
        c = np.where(c > 4080, ((w - np.arange(M, dtype=np.int64) * K1 - m * K4) * back) & (M - 1), c)
    return np.minimum(c, 4080)
def placed(u, d):
    c = (((d - K4) >> 1) * pow(K5 >> 1, 1023, 2048)) & 2047
    c = np.concatenate([c, c + 2048]); u = np.concatenate([u, u]); k = c <= 4080; c = c[k]; u = u[k]
    return ((u - c * K2) * pow(K1, 1023, M)) & (M - 1), c
def thrice():
    u = np.arange(M, dtype=np.int64); h = hit(u).astype(np.int16); us, ds = [], []
    for a in range(0, M // 2, 128):
        d = 2 * np.arange(a, a + 128, dtype=np.int64)[:, None] + 1; n = np.zeros((128, M), np.int8)
        for k in range(1, min(S, 8)): n += (h[(u + k * d) & (M - 1)] == h)
        j, i = np.nonzero(n >= 2); us.append(u[i]); ds.append(d[j, 0])
    return np.concatenate(us), np.concatenate(ds)
def twice():
    u = np.arange(M, dtype=np.int64); h = hit(u); n = np.zeros((M, M), np.int8)
    for m in range(S): n[h, ((u - h * K1 - m * K4) * pow(K2 + K5 * m, 1023, M)) & (M - 1)] += 1
    return np.nonzero(n[:, :4081] >= 2)
def some(rng, a):
    e = rng.permutation(len(a[0]))[:48]
    return a[0][e], a[1][e]
def setup_inputs(rng):
    s = states(rng); li = rng.random((N, 8, V)) < rng.choice(np.array([0.03, 0.1, 0.2, 0.35]), (N, 8, 1))
    return pack(lies(rng, s, li), li)
def setup_inputs_alike(rng):
    s = states(rng); li = rng.random((N, 8, V)) < 0.1; o = rng.permutation(8)
    for g in (o[0], o[1]): li[:, g] = False
    s = lies(rng, s, li)
    s[:, o[0]] = rng.integers(0, 256, (16, 1))
    s[:, o[1]] = rng.integers(0, 255, (16, 1)) + rng.integers(0, 2, (N, 16, V))
    s[:, o[2]] = 255 * rng.integers(0, 2, (N, 16, V))
    a = rng.integers(0, 256, (2, 16, 1)); s[:, o[3]] = np.where(rng.random((N, 1, V)) < 0.5, a[0], a[1])
    s[:, o[4]] = np.where(li[:, o[4]][:, None, :], s[:, o[4]], rng.integers(0, 256, (16, 1)))
    return pack(s, li)
def setup_inputs_ends(rng):
    s = states(rng); li = rng.random((N, 8, V)) < 0.1; s = lies(rng, s, li)
    k = rng.integers(0, 8, (N, 8, 1, V)); s = np.where(k == 0, 0, np.where(k == 1, 255, s))
    s[:, ::2, :, 0] = 255; s[:, 1::2, :, 0] = 0; s[:, ::2, :, V - 1] = 0; s[:, 1::2, :, V - 1] = 255
    li[0, :, 0] = True; li[N - 1, :, V - 1] = True; li[0, :, V - 1] = False; li[N - 1, :, 0] = False
    return pack(s, li)
def setup_inputs_liars(rng):
    s = states(rng); li = rng.random((N, 8, V)) < 0.25; o = rng.permutation(8)
    li[:, o[0]] = False; li[:, o[1]] = True
    i = int(rng.integers(0, M)); li[:, o[2]] = True; li[i // V, o[2], i % V] = False
    li[:, o[3]] = False; li[rng.integers(0, N), o[3], rng.integers(0, V)] = True
    li[:, o[4]] = False; li[rng.integers(0, N), o[4]] = True
    li[:, o[5]] = False; li[:, o[5], ::2] = True
    li[:, o[6]] = False; li[:, o[6], V // 4:V // 2] = True
    s = lies(rng, s, li)
    b = rng.integers(0, 256, 16); s[i // V, o[2], :, i % V] = b
    for p in draws(np.array([i]), np.array([int(np.sum(b))]), 0)[:, 0]: s[int(p) // V, o[2], :, int(p) % V] = b
    return pack(s, li)
def setup_inputs_steer(rng):
    o = rng.permutation(8); h = hit(np.arange(M, dtype=np.int64)); q = rng.permutation(N)
    c = rng.integers(0, 4081, (8, M)); li = rng.random((8, M)) < 0.1; li[o[0]] = False
    top = np.flatnonzero(np.bincount(h, minlength=M) >= 4)
    for g, m in ((o[0], 0), (o[1], S - 1), (o[2], int(rng.integers(0, S)))): c[g] = steered(rng, np.flatnonzero(h == rng.choice(top)), m)
    for g, w in ((o[3], q[0]), (o[4], q[1])): c[g] = steered(rng, np.flatnonzero(h // V == w), int(rng.integers(0, S)))
    self2 = twice(); three = placed(*thrice()); close = placed(np.arange(4, dtype=np.int64), np.ones(4, np.int64))
    for j in range(3):
        g = o[5 + j]; li[g] = rng.random(M) < 0.5
        a = [some(rng, close), some(rng, self2), some(rng, three)]
        for i, k in a[1:]:
            p = draws(i, k, 0); c[g, p] = rng.integers(0, 300, p.shape)
        p = draws(a[2][0], a[2][1], 0)[0]; c[g, p] = rng.integers(3600, 4081, p.shape)
        for i, k in a[j + 1:] + a[:j + 1]:
            c[g, i] = k; li[g, i] = False
    s = comps(rng, c)
    return pack(np.ascontiguousarray(s.reshape(8, 16, N, V).transpose(2, 0, 1, 3)), li.reshape(8, N, V).transpose(1, 0, 2))
def setup_inputs_spread(rng):
    s = np.floor(np.exp2(8 * rng.random((N, 8, 1, V))) * rng.random((N, 8, 16, V))).astype(np.int64)
    s = np.clip(np.where(rng.random((N, 8, 1, 1)) < 0.4, 255 - s, s), 0, 255)
    li = rng.random((N, 8, V)) < 0.5 * rng.random((N, 8, 1))
    q = rng.permutation(N); li[q[0]] = False; li[q[1]] = True
    return pack(s, li)
def check_inputs(d):
    bad = []
    v = d["x"].astype(np.float32)
    if not np.all((v >= 0) & (v <= 255) & (v == np.floor(v))): bad.append("range of x")
    if np.min(d["liar"]) < 0 or np.max(d["liar"]) > 1: bad.append("range of liar")
    return bad
def reference(x, liar):
    s = np.ascontiguousarray(x.astype(np.float32).astype(np.int32).reshape(N, 8, 16, V).transpose(1, 2, 0, 3)).reshape(8, 16, M)
    stay = np.ascontiguousarray(liar.transpose(1, 0, 2)).reshape(8, 1, M) == 1
    ids = np.arange(M, dtype=np.int64)
    for t in range(RO):
        c = np.add.reduce(s.astype(np.int64), axis=1)
        tot, hi, lo = 0, 0, 255
        for m in range(S):
            u = (ids * K1 + c * (K2 + K5 * m) + t * K3 + m * K4) & (M - 1)
            peer = ((u * u >> 7) + u) & (M - 1)
            v = np.take_along_axis(s, peer[:, None, :], 2)
            tot = tot + v; hi = np.maximum(hi, v); lo = np.minimum(lo, v)
        s = np.where(stay, s, (tot - hi - lo + P * s) >> SH)
    y = np.ascontiguousarray(s.reshape(8, 16, N, V).transpose(2, 0, 1, 3)).reshape(N, 128, V)
    return {"y": y.astype(np.float32).astype(BF)}

from concourse.bass import DstId, RemoteDMATransfer
from concourse.mybir import AluOpType as ALU, AxisListType, ActivationFunctionType as ACT

N, V, M, RO = 4, 1024, 4096, 6
K1, K2, K3, K4, K5 = 1597, 613, 911, 1223, 74
WW = 4864
MAGIC = 12582912.0
LIARBASE = 34 * 524288
ORDER = [3, 2, 1, 0]

CFG = {
    "up1": "dma",
    "dn1": "dma",
    "fin": "ssss",
    "split": (3,),
    "batch": ((3, 2), (1, 0)),
    "up0": "vvs", "dn0": "sv",
    "f": 1.25, "g": 1.56, "dma": 2.6, "slack": 0.05, "bc": (1.0, 1.0, -1.0, -1.0), "bo": (0.0, 0.0, 0.0, -1.0),
    "la": 6.5, "xa": 6.0,
}

SCRATCH = {
    "W0": ("sbuf", [128, WW], "bfloat16"), "W1": ("sbuf", [128, WW], "bfloat16"),
    "G0": ("sbuf", [128, 1024], "bfloat16"), "G1": ("sbuf", [128, 1024], "bfloat16"),
    "G2": ("sbuf", [128, 1024], "bfloat16"),
    "MX0": ("sbuf", [128, 1024], "bfloat16"), "MX1": ("sbuf", [128, 1024], "bfloat16"),
    "MN0": ("sbuf", [128, 1024], "bfloat16"), "MN1": ("sbuf", [128, 1024], "bfloat16"),
    "mxm": ("sbuf", [128, 1024], "bfloat16"), "mnm": ("sbuf", [128, 1024], "bfloat16"),
    "off0": ("sbuf", [128, 256], "uint16"), "off1": ("sbuf", [128, 256], "uint16"),
    "land": ("sbuf", [128, 1024], "bfloat16"),
    "SH": ("sbuf", [128, 320], "bfloat16"),
    "Iq": ("sbuf", [128, 128], "bfloat16"), "In": ("sbuf", [128, 128], "bfloat16"),
    "Ih": ("sbuf", [128, 128], "bfloat16"), "Ib": ("sbuf", [128, 128], "bfloat16"),
    "Im": ("sbuf", [128, 128], "bfloat16"),
    "ones": ("sbuf", [128, 256], "bfloat16"),
    "CW": ("sbuf", [128, 512], "bfloat16"), "LW": ("sbuf", [128, 512], "bfloat16"),
    "dg": ("sbuf", [128, 128], "bfloat16"), "m4": ("sbuf", [128, 128], "bfloat16"),
    "idf": ("sbuf", [128, 256], "float32"), "idn": ("sbuf", [128, 256], "float32"),
    "SP": ("sbuf", [128, 256], "float32"),
    "bhi": ("sbuf", [128, 256], "bfloat16"), "blo": ("sbuf", [128, 256], "bfloat16"),
    "pc": ("sbuf", [128, 8], "int32"), "ci": ("sbuf", [128, 8], "int32"), "cf": ("sbuf", [128, 24], "float32"),
    "vi": ("sbuf", [128, 256], "int32"), "ui": ("sbuf", [128, 256], "int32"), "xf": ("sbuf", [128, 256], "float32"),
    "xi": ("sbuf", [128, 256], "int32"), "pi": ("sbuf", [128, 256], "int32"),
    "li": ("sbuf", [128, 1024], "int32"), "lb": ("sbuf", [128, 1024], "bfloat16"),
    "DX": ("dram", [4, 128, 256], "bfloat16"),
    "DL": ("dram", [4, 128, 16], "int32"), "LL": ("dram", [4, 128, 16], "int32"),
    "acc0": ("psum", [128, 512], "float32"), "acc1": ("psum", [128, 512], "float32"),
    "acc2": ("psum", [128, 512], "float32"), "cps": ("psum", [128, 512], "float32"),
    "wt": ("psum", [128, 512], "float32"), "rp": ("psum", [128, 1536], "float32"),
}
SEMAPHORES = (["ev", "es", "et", "eg", "sent", "stx", "stl", "ownx"]
              + ["xa%d" % r for r in range(N)] + ["la%d" % r for r in range(N)] + ["ll%d" % r for r in range(N)]
              + ["ya%d" % r for r in range(N)] + ["st%d" % r for r in range(N)]
              + ["rd%d_%d" % (t, r) for t in range(RO) for r in range(N)])


def own(r):
    return 768 + 1024 * r


def hops(topo, a, b):
    ca, cb = topo.chip(a), topo.chip(b)
    return 1 if (topo.mates(ca, cb) or topo.same_plane(ca, cb)) else 2


def far_first(topo, cores, s):
    return sorted([d for d in range(N) if d != s], key=lambda d: (
        -hops(topo, cores[s], cores[d]), topo.mates(topo.chip(cores[s]), topo.chip(cores[d]))))


def masks(topo, cores, s):
    dsts = far_first(topo, cores, s)
    eng = [e for e in topo.engines(cores[s], cores[dsts[0]])
           if all(e in topo.engines(cores[s], cores[d]) for d in dsts)]
    h = len(eng) // 2
    return dict(zip(dsts, [eng[:h], eng[h:h + h // 2], eng[h + h // 2:]]))


def last_order(topo, cores, j):
    o = far_first(topo, cores, j)
    first = [d for d in o if d in CFG["batch"][0]]
    if not first:
        return o + [j]
    a = first[0] if (first[0] != o[2] or len(first) == 1) else first[1]
    return [a] + [d for d in o if d != a] + [j]


def rank_program(g, core, T, topo):
    rank = T.rank_of(core)
    if rank is None:
        return
    cores = list(T.cores)
    ops = []
    boost = [0.0]
    cyc = 0.83e-3 * CFG["f"]

    def rec(q, fn, c, r=(), w=(), x=(), dma=None, ext=(), remote=0, at=0.0, lat=0.0):
        ops.append({"q": q, "fn": fn, "c": c, "r": list(r), "w": list(w), "x": list(x), "dma": dma, "ext": list(ext),
                    "remote": remote, "at": at, "lat": lat, "boost": boost[0]})

    def vc(n):
        return 0.05 + max(n, 32) * cyc

    def vts(n, out, in0, s1, s2, op0, op1, r, w, x=()):
        if op1 is None:
            rec("v", lambda: g.vector.tensor_scalar(out, in0, s1, None, op0), vc(n), r, w, x)
        else:
            rec("v", lambda: g.vector.tensor_scalar(out, in0, s1, s2, op0, op1), vc(n), r, w, x)

    def vtt(n, out, a, b, op, r, w, x=()):
        rec("v", lambda: g.vector.tensor_tensor(out, a, b, op), vc(n), r, w, x)

    def vcp(n, out, a, r, w, x=()):
        rec("v", lambda: g.vector.tensor_copy(out, a), vc(n), r, w, x)

    def vset(n, ap, c, w, r=()):
        rec("v", lambda: g.vector.memset(ap, c), vc(n), r, w)

    def act(n, out, in_, r, w, x=(), **kw):
        rec("s", lambda: g.scalar.activation(out, in_, ACT.Identity, **kw), 0.015 + vc(n), r, w, x)

    def mm(n, out, lhsT, rhs, start, stop, r, bank):
        rec("t", lambda: g.tensor.matmul(out, lhsT, rhs, start, stop), 0.005 + max(n, 64) * cyc / 2, r, (), bank, lat=0.06)

    def dma(q, out, in_, r, w, sem, ext=(), at=0.0):
        eng = g.sync if q == "y" else g.scalar
        rec(q, lambda: eng.dma_start(out, in_), 0.06, r, w, (), sem, ext, at=at, lat=CFG["dma"])

    def cp(q, n, out, in_, r, w, x):
        if q == "v":
            vcp(n, out, in_, r, w, x)
        else:
            rec("s", lambda: g.scalar.activation(out, in_, ACT.Copy), 0.015 + vc(n), r, w, x)

    def iota(n, out, pat, base, cm, w, flt=True):
        if flt:
            rec("g", lambda: g.iota(out, pat, base, cm, allow_small_or_imprecise_dtypes=True), 0.1 + vc(2 * n), (), w)
        else:
            rec("g", lambda: g.iota(out, pat, base, cm), 0.1 + vc(2 * n), (), w)

    def send(d, dst, src, sem, r):
        rid, pid, _se = topo.addr(cores[d])
        rec("g", lambda: g.remote_dma(dst, src, T.sem[sem], T.sem.sent, pid, rid, topo.mask(core, cores[d])), 0.6, r,
            ["+remote"], remote=len(topo.engines(core, cores[d])), lat=5.0)

    W = [T.W0, T.W1]
    G = [T.G0, T.G1, T.G2]
    MX, MN = [T.MX0, T.MX1], [T.MN0, T.MN1]
    OFF = [T.off0, T.off1]
    ACC = [T.acc0, T.acc1, T.acc2]
    RPC = {"A": (0, 256, 512), "B": (1024, 1280, 768)}
    IDENT = T.SH[:, 96:224]
    others = far_first(topo, cores, rank)
    mine = masks(topo, cores, rank)

    def o(b, r, h="ab"):
        return ["W%d.o%d%s" % (b, r, c) for c in h]

    def allc(n):
        return ["%s%d" % (n, r) for r in range(N)]

    boost[0] = 20.0
    dma("y", T.DL[:], T.liar[:], (), ["DL"], "stl")
    boost[0] = 0.0
    for q in range(4):
        dma("y" if q % 2 else "s", T.DX[:, 32 * q:32 * q + 32, :], T.x[:, 256 * q:256 * q + 256], (), ["DX%d" % q], "stx")
    dma("s", T.li[0:8, 256 * rank:256 * rank + 256], T.liar[2 * rank:2 * rank + 2, :], (), ["li%d" % rank], "ll%d" % rank)
    iota(1, T.pc[:, 0:1], [[0, 1]], 0, 1, ["pc", "+remote"], False)
    iota(128, T.dg[:], [[1, 128]], 0, -1, ["dg", "+remote"])
    iota(256, T.idf[:], [[1024, 4], [4, 64]], 0, 0, ["idf", "+remote"])
    iota(128, T.m4[:], [[1, 32], [0, 4]], 0, 0, ["m4", "+remote"])

    def liars_out():
        trs = []
        for d in others:
            rid, pid, _se = topo.addr(cores[d])
            trs.append(RemoteDMATransfer(dst_ids=[DstId(rid=rid, pnc=pid)], dma_engine_mask=sum(1 << e for e in mine[d]),
                                         remote_sem=T.sem["la%d" % rank], src=T.DL[d], dst=T.LL[rank]))
        return g.remote_dma_fused(trs, local_sem=T.sem.sent)
    rec("g", liars_out, 0.6, ["DL"], ["+remote"], remote=sum(len(mine[d]) for d in others), lat=5.0)
    for d in others:
        send(d, T.W0[:, own(rank):own(rank) + 256], T.DX[d], "xa%d" % rank, allc("DX"))
    dma("y", T.W0[:, own(rank):own(rank) + 256], T.DX[rank], allc("DX"), o(0, rank), "ownx")
    for r in others:
        dma("y", T.li[0:8, 256 * r:256 * r + 256], T.LL[r], (), ["li%d" % r], "ll%d" % r,
            [("la%d" % r, len(masks(topo, cores, r)[rank]))], at=CFG["la"])

    ci, cf = T.ci, T.cf
    for c, sh, mask in ((0, 0, 3), (1, 2, 3), (2, 5, 3), (3, 4, 7), (4, 0, 4)):
        vts(1, ci[:, c:c + 1], T.pc[:, 0:1], sh, mask, ALU.logical_shift_right, ALU.bitwise_and, ["pc"], ["ci%d" % c])
    vset(160, T.SH[:], 0.0, ["SH"])
    vcp(5, cf[:, 0:5], ci[:, 0:5], ["ci%d" % c for c in range(5)], ["cf"])
    vset(128, T.ones[:], 1.0, ["ones"])
    KM, SHIFT, IDP, G4, C8, A, B = 5, 6, 7, 8, 9, 10, 11

    def col(c):
        return cf[:, c:c + 1]
    vts(1, col(IDP), col(2), 256.0, col(1), ALU.mult, ALU.add, ["cf"], ["idp"])
    for m in range(4):
        inv = pow(K2 + K5 * m, 1023, M)
        vts(1, col(12 + m), col(0), float(m), float(K1 * inv % M), ALU.is_equal, ALU.mult, ["cf"], ["a%d" % m])
        vts(1, col(16 + m), col(0), float(m), float(K4 * m * inv % M), ALU.is_equal, ALU.mult, ["cf"], ["b%d" % m])
    vts(64, IDENT, T.dg[:], 0.0, None, ALU.is_equal, None, ["dg", "SH"], ["SH"])
    rec("v", lambda: g.vector.tensor_reduce(col(A), cf[:, 12:16], AxisListType.X, ALU.add), vc(4), allc("a"), ["A"])
    rec("v", lambda: g.vector.tensor_reduce(col(B), cf[:, 16:20], AxisListType.X, ALU.add), vc(4), allc("b"), ["B"])
    vts(1, col(G4), col(3), 4.0, None, ALU.mult, None, ["cf"], ["g4"])
    vts(1, col(C8), col(0), 8.0, col(4), ALU.mult, ALU.add, ["cf"], ["c8"])
    vts(1, col(KM), col(0), float(K5), float(K2), ALU.mult, ALU.add, ["cf"], ["km"])
    vts(1, col(SHIFT), col(2), -256.0, 768.0, ALU.mult, ALU.add, ["cf"], ["shift"])
    act(256, T.idn[:], T.idf[:], ["idf", "idp"], ["idn"], bias=col(IDP))
    act(256, T.SP[:], T.idn[:], ["idn"], ["SP"], scale=128.0, bias=float(LIARBASE))
    for tile, name, s in ((T.Iq, "Iq", 0.25), (T.In, "In", -0.25), (T.Ih, "Ih", 0.5), (T.Ib, "Ib", -0.375), (T.Im, "Im", MAGIC)):
        act(128, tile[:], IDENT, ["SH"], [name], scale=s)
    vset(512, T.mxm[:], 0.0, ["mxm"])
    vset(128, T.mxm[:, 0:1024:4], -256.0, ["mxm"], ["mxm"])
    act(1024, T.mnm[:], T.mxm[:], ["mxm"], ["mnm"], scale=-1.0)
    vts(256, T.vi[:], T.idn[:], col(A), col(B), ALU.mult, ALU.add, ["idn", "A", "B"], allc("vi"))
    vts(256, T.ui[:], T.vi[:], 4080, None, ALU.bitwise_and, None, allc("vi"), allc("ui"))
    vts(256, T.xi[:], T.vi[:], 15, None, ALU.bitwise_and, None, allc("vi"), allc("xi"))
    vcp(256, T.bhi[:], T.ui[:], allc("ui"), ["bhi"])
    vcp(256, T.blo[:], T.xi[:], allc("xi"), ["blo"])
    for n in range(4):
        vts(64, T.CW[:, 128 * n:128 * n + 128], T.m4[:], col(G4), float(n), ALU.subtract, ALU.is_equal,
            ["m4", "g4"], ["CW%d" % n])
        vts(64, T.LW[:, 128 * n:128 * n + 128], T.m4[:], col(C8), float(n), ALU.subtract, ALU.is_equal,
            ["m4", "c8"], ["LW%d" % n])
    vset(384, T.W1[:, 4096:WW], 0.0, ["W1.b3U", "W1.b3D"])

    for r in [rank] + others:
        vcp(256, T.lb[0:8, 256 * r:256 * r + 256], T.li[0:8, 256 * r:256 * r + 256], ["li%d" % r], ["lb%d" % r])
        for n in range(4):
            mm(64, T.acc1[:, 64 * r:64 * r + 64], T.LW[0:8, 128 * n:128 * n + 128],
               T.lb[0:8, 256 * r + n:256 * r + 256:4], n == 0, n == 3, ["LW%d" % n, "lb%d" % r], ["acc1"])
    vtt(256, T.wt[:, 256:512], T.acc1[:, 0:256], T.SP[:], ALU.mult, ["SP"], ["T"], ["acc1", "wt"])

    def wall(b):
        return ([n for r in range(N) for n in o(b, r)]
                + ["W%d.b%d%s" % (b, k, s) for k in range(-1, N) for s in "UD"])

    def csum(b, r):
        out = T.cps[:, 64 * r:64 * r + 64]
        mm(64, out, IDENT, T.bhi[:, 64 * r:64 * r + 64], True, False, ["SH", "bhi"], ["cps"])
        mm(64, out, IDENT, T.blo[:, 64 * r:64 * r + 64], False, False, ["SH", "blo"], ["cps"])
        for n in range(4):
            mm(64, out, T.CW[:, 128 * n:128 * n + 128], W[b][:, own(r) + n:own(r) + 256:4], False, n == 3,
               ["CW%d" % n] + o(b, r), ["cps"])

    def offsets(t, chunks):
        a, n = 64 * min(chunks), 64 * len(chunks)
        s = slice(a, a + n)

        def nm(x):
            return ["%s%d" % (x, r) for r in chunks]
        vts(n, T.vi[:, s], T.cps[:, s], col(KM), float(K3 * t % M), ALU.mult, ALU.add, ["km"], nm("vi"), ["cps"])
        vts(n, T.ui[:, s], T.vi[:, s], M - 1, None, ALU.bitwise_and, None, nm("vi"), nm("ui"))
        vts(n, T.wt[:, s], T.ui[:, s], 128.0, None, ALU.add, None, nm("ui"), nm("w"), ["wt"])
        vtt(n, T.xf[:, s], T.wt[:, s], T.ui[:, s], ALU.mult, nm("w") + nm("ui"), nm("xf"), ["wt"])
        vtt(n, T.xi[:, s], T.xf[:, s], T.wt[:, 256 + a:256 + a + n], ALU.max, nm("xf") + ["T"], nm("xi"), ["wt"])
        vts(n, T.pi[:, s], T.xi[:, s], 7, M - 1, ALU.logical_shift_right, ALU.bitwise_and, nm("xi"), nm("pi"))
        vts(n, OFF[t % 2][:, s], T.pi[:, s], col(SHIFT), None, ALU.add, None, nm("pi") + ["shift"], nm("off%d." % (t % 2)))

    def banks(p, s):
        return ["rp%d" % (RPC[p][s - 1] // 512)]

    def half(lo, hi):
        return "ab" if hi - lo == 256 else ("a" if lo == 0 else "b")

    def pe_block(b, k, p, up, down, lo=0, hi=256, which=(1, 2, 3)):
        for s in which:
            out = T.rp[:, RPC[p][s - 1] + lo:RPC[p][s - 1] + hi]
            if up:
                mm(hi - lo, out, T.SH[:, 96 + 32 * s:224 + 32 * s], W[b][:, own(k) + lo:own(k) + hi], True, not down,
                   ["SH"] + o(b, k, half(lo, hi)), banks(p, s))
            if down:
                d = 32 * (s - 4)
                mm(hi - lo, out, T.SH[:, 96 + d:224 + d], W[b][:, own(k + 1) + lo:own(k + 1) + hi], not up, True,
                   ["SH"] + o(b, k + 1, half(lo, hi)), banks(p, s))

    def take_full(qs, b, k, p):
        c0 = own(k) + 256
        nm = ["W%d.b%dU" % (b, k), "W%d.b%dD" % (b, k)]
        cp(qs[0], 512, W[b][:, c0:c0 + 512], T.rp[:, RPC[p][0]:RPC[p][0] + 512], (), nm, banks(p, 1))
        cp(qs[1], 256, W[b][:, c0 + 512:c0 + 768], T.rp[:, RPC[p][2]:RPC[p][2] + 256], (), ["&" + n for n in nm], banks(p, 3))

    def take_up(qs, b, k, p):
        for s in (1, 2, 3):
            c0 = own(k) + 256 * s
            cp(qs[s - 1], 256, W[b][0:128 - 32 * s, c0:c0 + 256], T.rp[0:128 - 32 * s, RPC[p][s - 1]:RPC[p][s - 1] + 256], (),
               [("&" if s > 1 else "") + "W%d.b%dU" % (b, k)], banks(p, s))

    def dma_shift(b, r, t, up, down):
        sem = "rd%d_%d" % (t, r)
        c = own(r)
        for s in (1, 2, 3):
            if up:
                dma("y", W[b][0:128 - 32 * s, c + 256 * s:c + 256 * s + 256], W[b][32 * s:128, c:c + 256],
                    o(b, r), [("&" if s > 1 else "") + "W%d.b%dU" % (b, r)], sem)
            if down:
                dma("y", W[b][32 * s:128, c - 256 * s:c - 256 * s + 256], W[b][0:128 - 32 * s, c:c + 256],
                    o(b, r), [("&" if s > 1 else "") + "W%d.b%dD" % (b, r - 1)], sem)

    have, blocks, made = [], [], []
    for step, r in enumerate([rank] + others):
        if r != rank:
            rec("t", None, 0.0, (), o(0, r), ext=[("xa%d" % r, len(topo.engines(cores[r], core)))], at=CFG["xa"] + step)
        have.append(r)
        csum(0, r)
        for pair in ((3, 2), (1, 0)):
            if pair not in made and all(c in have for c in pair):
                made.append(pair)
                offsets(0, pair)
        new = [k for k in range(-1, N) if k not in blocks and all(c in have for c in (k, k + 1) if 0 <= c < N)]
        for k in new:
            p = "AB"[len(blocks) % 2]
            blocks.append(k)
            pe_block(0, k, p, k >= 0, k < N - 1)
            take_full("sv" if len(have) == N else "ss", 0, k, p)

    unit = 0
    for t in range(RO):
        b, nb = t % 2, (t + 1) % 2
        last = t == RO - 1
        order = last_order(topo, cores, rank) if last else ORDER
        for k in range(4):
            r = order[k]
            for lo, hi in (((0, 128), (128, 256)) if k in CFG["split"] else ((0, 256),)):
                n = hi - lo
                onv = CFG["fin"][k] == "v" and not last
                gi, ai = unit % 3, unit % 2
                unit += 1
                gt, acc, bank = G[gi], ACC[gi][:, 0:n], ["acc%d" % gi]
                win, off = W[b][:, 0:WW], OFF[b][:, 64 * r + lo // 4:64 * r + hi // 4]
                rec("s", lambda gt=gt, win=win, off=off, n=n: g.scalar.activation(gt[:, 0:4 * n], win.indirect(off), ACT.Copy),
                    0.065 + 4 * n * 0.83e-3 * CFG["g"], wall(b) + ["off%d.%d" % (b, r)], ["G%d" % gi])
                mm(n, acc, T.Ib[:], T.ones[:, 0:n], True, False, ["Ib", "ones"], bank)
                mm(n, acc, T.Ih[:], W[b][:, own(r) + lo:own(r) + hi], False, False, ["Ih"] + o(b, r), bank)
                for m in range(4):
                    mm(n, acc, T.Iq[:], gt[:, m:4 * n:4], False, False, ["Iq", "G%d" % gi], bank)
                for ext, msk, op, nm in ((MX[ai], T.mxm, ALU.max, "mx"), (MN[ai], T.mnm, ALU.min, "mn")):
                    rec("v", lambda ext=ext, msk=msk, gt=gt, op=op, n=n: g.vector.tensor_tensor_scan(
                        ext[:, 0:4 * n], msk[:, 0:4 * n], gt[:, 0:4 * n], 0.0, ALU.add, op), vc(2 * n),
                        [nm + "m", "G%d" % gi], ["%s%d" % (nm, ai)])
                    mm(n, acc, T.In[:], ext[:, 3:4 * n:4], False, onv and nm == "mn", ["In", "%s%d" % (nm, ai)], bank)
                out = W[nb][:, own(r) + lo:own(r) + hi]
                if onv:
                    vts(n, out, acc, MAGIC, MAGIC, ALU.add, ALU.subtract, (), o(nb, r, half(lo, hi)), bank)
                else:
                    mm(n, acc, T.Im[:], T.ones[:, 0:n], False, True, ["Im", "ones"], bank)
                    act(n, out, acc, (), o(nb, r, half(lo, hi)), bank, bias=-MAGIC)
                if k == 3 and not last:
                    for which in ((1, 2), (3,)):
                        pe_block(nb, -1, "A", False, True, lo, hi, which)
                        pe_block(nb, 0, "B", True, False, lo, hi, which)
            if last:
                if r != rank:
                    send(r, T.land[:, 256 * rank:256 * rank + 256], W[nb][:, own(r):own(r) + 256], "ya%d" % rank, o(nb, r))
                continue
            if k < 2:
                dma_shift(nb, r, t, True, True)
            elif k == 2:
                dma_shift(nb, r, t, CFG["up1"] == "dma", CFG["dn1"] == "dma")
                if CFG["dn1"] == "pe":
                    pe_block(nb, 0, "A", False, True)
                    take_full("ss", nb, 0, "A")
                if CFG["up1"] == "pe":
                    pe_block(nb, 1, "B", True, False)
                    take_up("sss", nb, 1, "B")
            else:
                take_full(CFG["dn0"], nb, -1, "A")
                take_up(CFG["up0"], nb, 0, "B")
            boost[0] = CFG["bc"][k]
            csum(nb, r)
            boost[0] = CFG["bo"][k]
            for batch in CFG["batch"]:
                if batch[-1] == r:
                    offsets(t + 1, batch)
            boost[0] = 0.0

    fb = RO % 2
    for j in range(N):
        for q in range(4):
            out = T.y[32 * j:32 * j + 32, 256 * q:256 * q + 256]
            if j == rank:
                dma("s", out, W[fb][32 * q:32 * q + 32, own(j):own(j) + 256], o(fb, j), (), "st%d" % j)
            else:
                dma("y", out, T.land[32 * q:32 * q + 32, 256 * j:256 * j + 256], (), (), "st%d" % j,
                    [("ya%d" % j, len(topo.engines(cores[j], core)))],
                    at=1000.0 + 10 * last_order(topo, cores, j).index(rank) + hops(topo, cores[j], core))

    emit(g, T, ops)


def depend(ops):
    writers, readers, before, bank, group = {}, {}, {}, {}, {}
    for i, o in enumerate(ops):
        if o["dma"]:
            group.setdefault(o["dma"], []).append(i)
    deps = []
    for i, o in enumerate(ops):
        q = o["q"]
        compute = not o["dma"] and not o["remote"]
        d = {}

        def add(j, read):
            p = ops[j]
            same = p["q"] == q and not p["dma"] and not p["remote"] and compute and p["fn"] is not None
            hard = not (same and (q == "t" or not read))
            for k in (group[p["dma"]] if p["dma"] and p["dma"] != o["dma"] else [j]):
                d[k] = d.get(k, False) or hard
        for n in o["r"]:
            for j in writers.get(n, []):
                add(j, True)
        for n in o["w"]:
            if n[0] == "+":
                for j in writers.get(n, []):
                    d.setdefault(j, False)
                writers[n] = [i]
            elif n[0] == "&":
                for j in before[n[1:]]:
                    add(j, False)
                writers[n[1:]].append(i)
            else:
                before[n] = [j for j in readers.get(n, []) + writers.get(n, []) if j != i]
                for j in before[n]:
                    add(j, False)
                writers[n] = [i]
                readers[n] = []
        for n in o["x"]:
            for j in bank.get(n, {}).values():
                add(j, False)
            bank.setdefault(n, {})[q] = i
        for n in o["r"]:
            if n not in o["w"]:
                readers.setdefault(n, []).append(i)
        deps.append(d)
    return deps


def arrange(ops, deps):
    n = len(ops)
    after = [[] for _ in range(n)]
    for i in range(n):
        for j in deps[i]:
            after[j].append(i)
    level = [0.0] * n
    for i in range(n - 1, -1, -1):
        level[i] = ops[i]["c"] + ops[i]["lat"] + max([level[k] + 0.08 for k in after[i] if k > i] + [0.0])
    level = [level[i] + ops[i]["boost"] for i in range(n)]
    left = [len(deps[i]) for i in range(n)]
    ready = {q: [] for q in "vstyg"}
    start = [o["at"] for o in ops]
    for i in range(n):
        if left[i] == 0:
            ready[ops[i]["q"]].append(i)
    free = {q: 0.0 for q in "vstyg"}
    order = []
    while len(order) < n:
        best = None
        for q in ready:
            if ready[q]:
                t0 = max(free[q], min(start[i] for i in ready[q]))
                i = max([i for i in ready[q] if start[i] <= t0 + CFG["slack"]], key=lambda i: (level[i], -i))
                t = max(free[q], start[i])
                if best is None or t < best[0]:
                    best = (t, i)
        t, i = best
        q = ops[i]["q"]
        ready[q].remove(i)
        order.append(i)
        free[q] = t + ops[i]["c"]
        for k in after[i]:
            hard = deps[k][i]
            start[k] = max(start[k], free[q] + (ops[i]["lat"] + (0.04 if ops[k]["q"] == q else 0.08) if hard else 0.0))
            left[k] -= 1
            if left[k] == 0:
                ready[ops[k]["q"]].append(k)
    return order


def emit(g, T, ops):
    queue = {"v": g.vector, "s": g.scalar, "t": g.tensor, "y": g.sync, "g": g}
    esem = {"v": "ev", "s": "es", "t": "et", "g": "eg"}
    deps = depend(ops)
    total = {}
    for o in ops:
        if o["dma"]:
            total[o["dma"]] = total.get(o["dma"], 0) + 16
    count = {}
    clock = {q: {} for q in queue}
    snap, event = {}, {}
    sent = 0

    def wait(q, sem, val):
        if clock[q].get(sem, 0) >= val:
            return
        queue[q].wait_ge(T.sem[sem], val)
        clock[q][sem] = val
        for s, v in snap.get((sem, val), {}).items():
            if clock[q].get(s, 0) < v:
                clock[q][s] = v

    for i in arrange(ops, deps):
        o = ops[i]
        q = o["q"]
        if o["fn"] is None:
            event[i] = o["ext"]
            continue
        need = {}
        for sem, val in o["ext"] + [ev for j, hard in deps[i].items() if hard for ev in event[j]]:
            need[sem] = max(need.get(sem, 0), val)
        for sem, val in sorted(need.items(), key=lambda e: (e[0] == esem.get(q), -len(snap.get(e, {})))):
            wait(q, sem, val)
        ins = o["fn"]()
        if o["remote"]:
            sent += o["remote"]
            event[i] = []
            continue
        if o["dma"]:
            ins.then_inc(T.sem[o["dma"]], 16)
            ev = (o["dma"], total[o["dma"]])
        else:
            ins.then_inc(T.sem[esem[q]], 1)
            count[q] = count.get(q, 0) + 1
            ev = (esem[q], count[q])
        old = snap.get(ev, {})
        snap[ev] = {s: max(old.get(s, 0), clock[q].get(s, 0)) for s in set(old) | set(clock[q])}
        event[i] = [ev]
    for q, n in count.items():
        wait("g", esem[q], n)
    for sem, val in total.items():
        wait("g", sem, val)
    wait("g", "sent", sent)
